import numpy as np
import ml_dtypes


def mxq(x, axis, fmt="e4m3"):
    dtype, down = {"e4m3": (ml_dtypes.float8_e4m3fn, 7), "e5m2": (ml_dtypes.float8_e5m2, 14)}[fmt]
    v = np.moveaxis(np.asarray(x, np.float32).astype(ml_dtypes.bfloat16).astype(np.float64), axis, -1)
    blocks = v.reshape(v.shape[:-1] + (-1, 32))
    amax = np.abs(blocks).max(-1, keepdims=True)
    byte = np.maximum(np.where(amax > 0, np.frexp(amax)[1] - 1 + 127, 0) - down, 1)
    scale = np.exp2(byte - 127.0)
    codes = (blocks / scale).astype(np.float32).astype(dtype).astype(np.float64)
    return np.moveaxis((codes * scale).reshape(v.shape), -1, axis)


WIDE = False


def mx_kscale(k):
    if not WIDE:
        return np.ones(k)
    levels = np.array([10, -10, 5, -5, 0])
    if k % 512:
        return np.exp2(np.random.permutation(np.resize(levels, k // 32))).repeat(32)
    a = np.empty((k // 512, 16))
    for p in range(k // 512):
        a[p, :8] = np.random.permutation(np.resize(levels, 8))
        for g in range(8):
            far = levels[np.abs(levels - a[p, g]) >= 10]
            a[p, g + 8] = far[np.random.randint(len(far))]
    return np.exp2(a.ravel()).repeat(32)


def f64(x):
    return np.asarray(x).astype(np.float64)


def striped(idx):
    return np.tile(idx.reshape(-1, 16).T, (8, 1)).astype(np.uint16)


def unstriped(offs):
    return offs[:16].T.reshape(-1).astype(np.int64)


E2M1 = np.array([0.0, 0.5, 1.0, 1.5, 2.0, 3.0, 4.0, 6.0, -0.0, -0.5, -1.0, -1.5, -2.0, -3.0, -4.0, -6.0])


def pack_weight(w, fmt):
    k, n = w.shape
    w = f64(np.asarray(w, np.float32).astype(ml_dtypes.bfloat16)).reshape(k // 32, 32, n)
    amax = np.abs(w).max(1)
    if fmt == "e4m3":
        byte = np.frexp(amax)[1] - 1 + 127 - 7
    else:
        mant, ex = np.frexp(amax / 6.0)
        byte = np.where(mant > 0.5, ex, ex - 1) + 127
    byte = np.clip(np.where(amax > 0, byte, 1), 1, 254)
    scaled = (w * np.exp2(127.0 - byte)[:, None, :]).reshape(k, n).astype(np.float32)
    by_word = np.ascontiguousarray(scaled.reshape(k // 512, 128, 4, n).transpose(0, 1, 3, 2))
    if fmt == "e4m3":
        words = by_word.astype(ml_dtypes.float8_e4m3fn).view(np.uint8)
    else:
        c = by_word.astype(ml_dtypes.float4_e2m1fn).view(np.uint8) & 0xF
        words = (c[..., 0::2] | (c[..., 1::2] << 4)).reshape(k // 512, 128, 2 * n)
    return np.ascontiguousarray(words), np.ascontiguousarray(byte.astype(np.uint8).reshape(k // 512, 16, n))


def unpack_weight(words, scales, fmt):
    g, _, n = scales.shape
    words = np.ascontiguousarray(words).reshape(g, 128, n, -1)
    if fmt == "e4m3":
        vals = words.view(ml_dtypes.float8_e4m3fn).astype(np.float64)
    else:
        nib = np.empty((g, 128, n, 4), np.uint8)
        nib[..., 0::2] = words & 0xF
        nib[..., 1::2] = words >> 4
        vals = E2M1[nib]
    vals = vals * np.repeat(np.exp2(scales.astype(np.float64) - 127.0), 8, axis=1)[..., None]
    return vals.transpose(0, 1, 3, 2).reshape(g * 512, n)


def pack_table(v):
    words, scales = pack_weight(v, "e4m3")
    return np.concatenate([words.reshape(words.shape[0], -1), scales.reshape(scales.shape[0], -1)], axis=1)


def unpack_table(tab):
    g, t = tab.shape[0], tab.shape[1] // 528
    return unpack_weight(tab[:, :512 * t].reshape(g, 128, t, 4), tab[:, 512 * t:].reshape(g, 16, t), "e4m3")


K, L, M, T, S = 512, 512, 128, 4096, 2048


def setup_inputs():
    n = np.random.standard_normal
    s1 = mx_kscale(K)[:, None]
    s2 = mx_kscale(L)[:, None]
    p_w4 = pack_weight(n((K, M)) / np.sqrt(K) / s1, "e2m1")
    return {
        "tab": pack_table(n((K, T)) * s1),
        "w4_words": p_w4[0],
        "w4_scales": p_w4[1],
        "x": (n((L, S)) * s2).astype(np.float32),
        "u": (n((L, M)) / np.sqrt(L) / s2).astype(np.float32),
        "offs": striped(np.random.permutation(T)[:S]),
    }


def reference(tab, w4_words, w4_scales, x, u, offs):
    tab_ = unpack_table(tab)[:, unstriped(offs)]
    w4_ = unpack_weight(w4_words, w4_scales, "e2m1")
    x_ = mxq(f64(x), 0, "e4m3")
    u_ = mxq(f64(u), 0, "e4m3")
    y = w4_.T @ tab_ + u_.T @ x_
    return y

@@ -1,0 +1,172 @@
+from contextlib import ExitStack
+
+import concourse.mybir as mybir
+
+K, L, M, T, S = 512, 512, 128, 4096, 2048
+FLOPS = 2 * (K + L) * M * S
+
+F32 = mybir.dt.float32
+BF16 = mybir.dt.bfloat16
+I32 = mybir.dt.int32
+U32 = mybir.dt.uint32
+U16 = mybir.dt.uint16
+U8 = mybir.dt.uint8
+FP8X4 = mybir.dt.float8_e4m3fn_x4
+FP4X4 = mybir.dt.float4_e2m1fn_x4
+
+P = 128
+PACK = 4
+CHUNK = 256
+GROUPS = [(0, 512), (512, 512), (1024, 512), (1536, 128), (1664, 128), (1792, 128), (1920, 128)]
+LAST_SPLIT = 176
+
+
+def tile_list_tabx_none_kernel(tc, tab, w4_words, w4_scales, x, u, offs, out):
+    nc = tc.nc
+    with ExitStack() as ctx:
+        keep = ctx.enter_context(tc.tile_pool(name="keep", bufs=1))
+        psum = ctx.enter_context(tc.psum_pool(name="psum", bufs=1))
+
+        offsets = keep.tile([P, S // 16], U16, name="offsets")
+        tab_words = keep.tile([P, T], I32, name="tab_words", align_bytes=64)
+        tab_scales = keep.tile([P, T // 4], I32, name="tab_scales", align_bytes=64)
+        w4_codes = keep.tile([P, M // 2], I32, name="w4_codes", align_bytes=64)
+        w4_plane = keep.tile([P, M // 4], I32, name="w4_plane", align_bytes=64)
+        u_raw = keep.tile([P, PACK, M], F32, name="u_raw", align_bytes=64)
+        u_bf = keep.tile([P, M, PACK], BF16, name="u_bf", align_bytes=64)
+        u_codes = keep.tile([P, M], U32, name="u_codes", align_bytes=64)
+        u_plane = keep.tile([P, M], U8, name="u_plane", align_bytes=64)
+        x_raw = [keep.tile([P, PACK, CHUNK], F32, name=f"x_raw{c}", align_bytes=64) for c in range(S // CHUNK)]
+        x_bf = keep.tile([P, S, PACK], BF16, name="x_bf", align_bytes=64)
+        x_codes = keep.tile([P, S], U32, name="x_codes", align_bytes=64)
+        x_plane = keep.tile([P, S], U8, name="x_plane", align_bytes=64)
+        v_codes = keep.tile([P, S], U32, name="v_codes", align_bytes=64)
+        v_plane = keep.tile([P, S], U8, name="v_plane", align_bytes=64)
+        result = keep.tile([P, S], F32, name="result", align_bytes=64)
+        acc = [psum.tile([P, width], F32, name=f"acc{g}") for g, (first, width) in enumerate(GROUPS)]
+
+        x_rows = x.rearrange("(p j) s -> p j s", j=PACK)
+        words_hbm = tab[0, 0 : K * T].rearrange("(p b) -> p b", p=P).bitcast(I32)
+        scales_hbm = tab[0, K * T : K * T + 16 * T].rearrange("(q r t) -> r q t", q=4, r=4).bitcast(I32)
+        w4_scales_hbm = w4_scales[0].rearrange("(q r) n -> r q n", r=4).bitcast(I32)
+
+        def load_x(c):
+            nc.sync.dma_start(out=x_raw[c][:], in_=x_rows[:, :, c * CHUNK : (c + 1) * CHUNK])
+
+        def interleave(copy, dst, src):
+            copy(
+                out=dst.rearrange("p (c i) t -> p c t i", i=4),
+                in_=src.rearrange("p t (c i) -> p c t i", i=4),
+            )
+
+        def cast_x(copy, c, lo=0, hi=CHUNK):
+            interleave(copy, x_bf[:, c * CHUNK + lo : c * CHUNK + hi, :], x_raw[c][:, :, lo:hi])
+
+        def quantize_x(first, width):
+            cols = slice(first, first + width)
+            nc.vector.quantize_mx(
+                out=x_codes[:, cols].bitcast(FP8X4),
+                scales=x_plane[:, cols],
+                in_=x_bf[:, cols, :].rearrange("p w t -> p (w t)"),
+            )
+
+        def table_pass(g):
+            first, width = GROUPS[g]
+            cols = slice(first, first + width)
+            nc.tensor.matmul_mx(
+                out=acc[g][:],
+                lhsT=w4_codes[:].bitcast(U8).bitcast(FP4X4),
+                lhsT_scale=w4_plane[:].bitcast(U8),
+                rhs=v_codes[:, cols].bitcast(FP8X4),
+                rhs_scale=v_plane[:, cols],
+                start=True,
+                stop=False,
+            )
+
+        def x_pass(g):
+            first, width = GROUPS[g]
+            cols = slice(first, first + width)
+            nc.tensor.matmul_mx(
+                out=acc[g][:],
+                lhsT=u_codes[:].bitcast(FP8X4),
+                lhsT_scale=u_plane[:],
+                rhs=x_codes[:, cols].bitcast(FP8X4),
+                rhs_scale=x_plane[:, cols],
+                start=False,
+                stop=True,
+            )
+
+        def empty(copy, g):
+            first, width = GROUPS[g]
+            copy(out=result[:, first : first + width], in_=acc[g][:])
+
+        def store(first, width):
+            nc.sync.dma_start(out=out[:, first : first + width], in_=result[:, first : first + width])
+
+        on_vector = nc.vector.tensor_copy
+        on_scalar = nc.scalar.copy
+
+        nc.vector.memset(tab_scales[:], 0)
+        nc.vector.memset(w4_plane[:], 0)
+
+        nc.sync.dma_start(offsets[:], offs)
+        nc.sync.dma_start(out=u_raw[:], in_=u.rearrange("(p j) n -> p j n", j=PACK))
+        for r in range(4):
+            nc.sync.dma_start(out=tab_scales[r:P:32, :], in_=scales_hbm[r])
+        load_x(0)
+        nc.sync.dma_start(out=tab_words[:], in_=words_hbm)
+        load_x(1)
+        load_x(2)
+        nc.sync.dma_start(out=w4_codes[:], in_=w4_words[0].bitcast(I32))
+        for r in range(4):
+            nc.sync.dma_start(out=w4_plane[r:P:32, :], in_=w4_scales_hbm[r])
+        for c in range(3, S // CHUNK):
+            load_x(c)
+
+        nc.vector.tensor_copy(v_plane[:], tab_scales[:].bitcast(U8).indirect(offsets[:]))
+        interleave(on_scalar, u_bf[:], u_raw[:])
+        cast_x(on_scalar, 0)
+        nc.vector.quantize_mx(
+            out=u_codes[:].bitcast(FP8X4), scales=u_plane[:], in_=u_bf[:].rearrange("p w t -> p (w t)")
+        )
+        quantize_x(0, 256)
+        for h in range(2):
+            nc.vector.tensor_copy(
+                v_codes[:, h * 1024 : (h + 1) * 1024],
+                tab_words[:].bitcast(U32).indirect(offsets[:, h * 64 : (h + 1) * 64]),
+            )
+        for g in range(len(GROUPS)):
+            table_pass(g)
+
+        for c in (1, 2, 3):
+            cast_x(on_scalar, c)
+        quantize_x(256, 256)
+        x_pass(0)
+        quantize_x(512, 512)
+        x_pass(1)
+        cast_x(on_scalar, 4)
+        empty(on_scalar, 0)
+        store(0, 512)
+        cast_x(on_scalar, 5)
+        empty(on_scalar, 1)
+        store(512, 512)
+        cast_x(on_vector, 6)
+        quantize_x(1024, 512)
+        x_pass(2)
+        quantize_x(1536, 256)
+        x_pass(3)
+        x_pass(4)
+        empty(on_vector, 2)
+        store(1024, 512)
+        cast_x(on_vector, 7, 0, LAST_SPLIT)
+        cast_x(on_scalar, 7, LAST_SPLIT, CHUNK)
+        empty(on_vector, 3)
+        empty(on_scalar, 4)
+        store(1536, 256)
+        quantize_x(1792, 128)
+        x_pass(5)
+        quantize_x(1920, 128)
+        x_pass(6)
+        empty(on_scalar, 5)
+        empty(on_vector, 6)
+        store(1792, 256)

@@ -36,7 +36,8 @@ def tile_list_tabx_none_kernel(tc, tab, w4_words, w4_scales, x, u, offs, out):
         u_bf = keep.tile([P, M, PACK], BF16, name="u_bf", align_bytes=64)
         u_codes = keep.tile([P, M], U32, name="u_codes", align_bytes=64)
         u_plane = keep.tile([P, M], U8, name="u_plane", align_bytes=64)
-        x_raw = [keep.tile([P, PACK, CHUNK], F32, name=f"x_raw{c}", align_bytes=64) for c in range(S // CHUNK)]
+        x_all = keep.tile([P, S // CHUNK, PACK, CHUNK], F32, name="x_all", align_bytes=64)
+        x_raw = [x_all[:, c] for c in range(S // CHUNK)]
         x_bf = keep.tile([P, S, PACK], BF16, name="x_bf", align_bytes=64)
         x_codes = keep.tile([P, S], U32, name="x_codes", align_bytes=64)
         x_plane = keep.tile([P, S], U8, name="x_plane", align_bytes=64)
@@ -51,7 +52,7 @@ def tile_list_tabx_none_kernel(tc, tab, w4_words, w4_scales, x, u, offs, out):
         w4_scales_hbm = w4_scales[0].rearrange("(q r) n -> r q n", r=4).bitcast(I32)
 
         def load_x(c):
-            nc.sync.dma_start(out=x_raw[c][:], in_=x_rows[:, :, c * CHUNK : (c + 1) * CHUNK])
+            nc.sync.dma_start(out=x_raw[c], in_=x_rows[:, :, c * CHUNK : (c + 1) * CHUNK])
 
         def interleave(copy, dst, src):
             copy(
@@ -107,66 +108,66 @@ def tile_list_tabx_none_kernel(tc, tab, w4_words, w4_scales, x, u, offs, out):
         on_scalar = nc.scalar.copy
 
         nc.vector.memset(tab_scales[:], 0)
+        nc.vector.memset(tab_words[:, 0:8], 0)
+        nc.vector.memset(x_all[:, :, 0, 0:8], 0.0)
         nc.vector.memset(w4_plane[:], 0)
 
         nc.sync.dma_start(offsets[:], offs)
         nc.sync.dma_start(out=u_raw[:], in_=u.rearrange("(p j) n -> p j n", j=PACK))
-        for r in range(4):
-            nc.sync.dma_start(out=tab_scales[r:P:32, :], in_=scales_hbm[r])
-        load_x(0)
-        nc.sync.dma_start(out=tab_words[:], in_=words_hbm)
-        load_x(1)
-        load_x(2)
         nc.sync.dma_start(out=w4_codes[:], in_=w4_words[0].bitcast(I32))
         for r in range(4):
+            nc.sync.dma_start(out=tab_scales[r:P:32, :], in_=scales_hbm[r])
+        nc.sync.dma_start(out=tab_words[:], in_=words_hbm)
+        load_x(0)
+        for r in range(4):
             nc.sync.dma_start(out=w4_plane[r:P:32, :], in_=w4_scales_hbm[r])
-        for c in range(3, S // CHUNK):
+        for c in range(1, S // CHUNK):
             load_x(c)
 
         nc.vector.tensor_copy(v_plane[:], tab_scales[:].bitcast(U8).indirect(offsets[:]))
         interleave(on_scalar, u_bf[:], u_raw[:])
-        cast_x(on_scalar, 0)
         nc.vector.quantize_mx(
             out=u_codes[:].bitcast(FP8X4), scales=u_plane[:], in_=u_bf[:].rearrange("p w t -> p (w t)")
         )
-        quantize_x(0, 256)
-        for h in range(2):
-            nc.vector.tensor_copy(
-                v_codes[:, h * 1024 : (h + 1) * 1024],
-                tab_words[:].bitcast(U32).indirect(offsets[:, h * 64 : (h + 1) * 64]),
-            )
-        for g in range(len(GROUPS)):
-            table_pass(g)
 
-        for c in (1, 2, 3):
+        def gather_words(h):
+            nc.vector.tensor_copy(
+                v_codes[:, h * 512 : (h + 1) * 512],
+                tab_words[:].bitcast(U32).indirect(offsets[:, h * 32 : (h + 1) * 32]),
+            )
+
+        for h in range(3):
+            gather_words(h)
+            table_pass(h)
+        for c in range(7):
             cast_x(on_scalar, c)
-        quantize_x(256, 256)
+        quantize_x(0, 512)
         x_pass(0)
+        gather_words(3)
+        for g in range(3, 7):
+            table_pass(g)
+        empty(on_vector, 0)
+        store(0, 512)
         quantize_x(512, 512)
         x_pass(1)
-        cast_x(on_scalar, 4)
-        empty(on_scalar, 0)
-        store(0, 512)
-        cast_x(on_scalar, 5)
-        empty(on_scalar, 1)
+        quantize_x(1024, 256)
+        empty(on_vector, 1)
         store(512, 512)
-        cast_x(on_vector, 6)
-        quantize_x(1024, 512)
+        quantize_x(1280, 256)
         x_pass(2)
+        cast_x(on_vector, 7, 0, LAST_SPLIT)
+        cast_x(on_scalar, 7, LAST_SPLIT, CHUNK)
         quantize_x(1536, 256)
         x_pass(3)
         x_pass(4)
-        empty(on_vector, 2)
-        store(1024, 512)
-        cast_x(on_vector, 7, 0, LAST_SPLIT)
-        cast_x(on_scalar, 7, LAST_SPLIT, CHUNK)
-        empty(on_vector, 3)
-        empty(on_scalar, 4)
-        store(1536, 256)
-        quantize_x(1792, 128)
+        quantize_x(1792, 256)
         x_pass(5)
-        quantize_x(1920, 128)
         x_pass(6)
+        empty(on_scalar, 2)
+        store(1024, 512)
+        empty(on_scalar, 3)
+        empty(on_vector, 4)
+        store(1536, 256)
         empty(on_scalar, 5)
         empty(on_vector, 6)
         store(1792, 256)

@@ -16,9 +16,10 @@ FP4X4 = mybir.dt.float4_e2m1fn_x4
 
 P = 128
 PACK = 4
-CHUNK = 256
-GROUPS = [(0, 512), (512, 512), (1024, 512), (1536, 128), (1664, 128), (1792, 128), (1920, 128)]
-LAST_SPLIT = 176
+CHUNKS = [(0, 256), (256, 256), (512, 256), (768, 256), (1024, 256), (1280, 256), (1536, 256), (1792, 128), (1920, 128)]
+BANKS = [(0, 512), (512, 512), (1024, 256), (1280, 256), (1536, 128), (1664, 128), (1792, 128), (1920, 128)]
+LAST_SPLIT = 80
+STAGE = [4 * 768, 4 * 1024, 4 * 1920, 4 * 1920 + 256, 4 * 1536, 4 * 1536 + 128, 4 * 1792, 4 * 1792 + 128]
 
 
 def tile_list_tabx_none_kernel(tc, tab, w4_words, w4_scales, x, u, offs, out):
@@ -36,15 +37,17 @@ def tile_list_tabx_none_kernel(tc, tab, w4_words, w4_scales, x, u, offs, out):
         u_bf = keep.tile([P, M, PACK], BF16, name="u_bf", align_bytes=64)
         u_codes = keep.tile([P, M], U32, name="u_codes", align_bytes=64)
         u_plane = keep.tile([P, M], U8, name="u_plane", align_bytes=64)
-        x_all = keep.tile([P, S // CHUNK, PACK, CHUNK], F32, name="x_all", align_bytes=64)
-        x_raw = [x_all[:, c] for c in range(S // CHUNK)]
+        x_all = keep.tile([P, PACK * S], F32, name="x_all", align_bytes=64)
+        x_raw = [
+            x_all[:, PACK * first : PACK * (first + width)].rearrange("p (j s) -> p j s", j=PACK)
+            for first, width in CHUNKS
+        ]
         x_bf = keep.tile([P, S, PACK], BF16, name="x_bf", align_bytes=64)
         x_codes = keep.tile([P, S], U32, name="x_codes", align_bytes=64)
         x_plane = keep.tile([P, S], U8, name="x_plane", align_bytes=64)
         v_codes = keep.tile([P, S], U32, name="v_codes", align_bytes=64)
         v_plane = keep.tile([P, S], U8, name="v_plane", align_bytes=64)
-        result = keep.tile([P, S], F32, name="result", align_bytes=64)
-        acc = [psum.tile([P, width], F32, name=f"acc{g}") for g, (first, width) in enumerate(GROUPS)]
+        acc = [psum.tile([P, width], F32, name=f"acc{g}") for g, (first, width) in enumerate(BANKS)]
 
         x_rows = x.rearrange("(p j) s -> p j s", j=PACK)
         words_hbm = tab[0, 0 : K * T].rearrange("(p b) -> p b", p=P).bitcast(I32)
@@ -52,7 +55,8 @@ def tile_list_tabx_none_kernel(tc, tab, w4_words, w4_scales, x, u, offs, out):
         w4_scales_hbm = w4_scales[0].rearrange("(q r) n -> r q n", r=4).bitcast(I32)
 
         def load_x(c):
-            nc.sync.dma_start(out=x_raw[c], in_=x_rows[:, :, c * CHUNK : (c + 1) * CHUNK])
+            first, width = CHUNKS[c]
+            nc.sync.dma_start(out=x_raw[c], in_=x_rows[:, :, first : first + width])
 
         def interleave(copy, dst, src):
             copy(
@@ -60,8 +64,10 @@ def tile_list_tabx_none_kernel(tc, tab, w4_words, w4_scales, x, u, offs, out):
                 in_=src.rearrange("p t (c i) -> p c t i", i=4),
             )
 
-        def cast_x(copy, c, lo=0, hi=CHUNK):
-            interleave(copy, x_bf[:, c * CHUNK + lo : c * CHUNK + hi, :], x_raw[c][:, :, lo:hi])
+        def cast_x(copy, c, lo=0, hi=None):
+            first, width = CHUNKS[c]
+            hi = width if hi is None else hi
+            interleave(copy, x_bf[:, first + lo : first + hi, :], x_raw[c][:, :, lo:hi])
 
         def quantize_x(first, width):
             cols = slice(first, first + width)
@@ -71,11 +77,12 @@ def tile_list_tabx_none_kernel(tc, tab, w4_words, w4_scales, x, u, offs, out):
                 in_=x_bf[:, cols, :].rearrange("p w t -> p (w t)"),
             )
 
-        def table_pass(g):
-            first, width = GROUPS[g]
-            cols = slice(first, first + width)
+        def table_pass(g, lo=0, hi=None):
+            first, width = BANKS[g]
+            hi = width if hi is None else hi
+            cols = slice(first + lo, first + hi)
             nc.tensor.matmul_mx(
-                out=acc[g][:],
+                out=acc[g][:, lo:hi],
                 lhsT=w4_codes[:].bitcast(U8).bitcast(FP4X4),
                 lhsT_scale=w4_plane[:].bitcast(U8),
                 rhs=v_codes[:, cols].bitcast(FP8X4),
@@ -84,11 +91,12 @@ def tile_list_tabx_none_kernel(tc, tab, w4_words, w4_scales, x, u, offs, out):
                 stop=False,
             )
 
-        def x_pass(g):
-            first, width = GROUPS[g]
-            cols = slice(first, first + width)
+        def x_pass(g, lo=0, hi=None):
+            first, width = BANKS[g]
+            hi = width if hi is None else hi
+            cols = slice(first + lo, first + hi)
             nc.tensor.matmul_mx(
-                out=acc[g][:],
+                out=acc[g][:, lo:hi],
                 lhsT=u_codes[:].bitcast(FP8X4),
                 lhsT_scale=u_plane[:],
                 rhs=x_codes[:, cols].bitcast(FP8X4),
@@ -98,18 +106,19 @@ def tile_list_tabx_none_kernel(tc, tab, w4_words, w4_scales, x, u, offs, out):
             )
 
         def empty(copy, g):
-            first, width = GROUPS[g]
-            copy(out=result[:, first : first + width], in_=acc[g][:])
+            first, width = BANKS[g]
+            copy(out=x_all[:, STAGE[g] : STAGE[g] + width], in_=acc[g][:])
 
-        def store(first, width):
-            nc.sync.dma_start(out=out[:, first : first + width], in_=result[:, first : first + width])
+        def store(g, width):
+            first = BANKS[g][0]
+            nc.sync.dma_start(out=out[:, first : first + width], in_=x_all[:, STAGE[g] : STAGE[g] + width])
 
         on_vector = nc.vector.tensor_copy
         on_scalar = nc.scalar.copy
 
         nc.vector.memset(tab_scales[:], 0)
         nc.vector.memset(tab_words[:, 0:8], 0)
-        nc.vector.memset(x_all[:, :, 0, 0:8], 0.0)
+        nc.vector.memset(x_all[:].rearrange("p (c s) -> p c s", s=512)[:, :, 0:8], 0.0)
         nc.vector.memset(w4_plane[:], 0)
 
         nc.sync.dma_start(offsets[:], offs)
@@ -121,7 +130,7 @@ def tile_list_tabx_none_kernel(tc, tab, w4_words, w4_scales, x, u, offs, out):
         load_x(0)
         for r in range(4):
             nc.sync.dma_start(out=w4_plane[r:P:32, :], in_=w4_scales_hbm[r])
-        for c in range(1, S // CHUNK):
+        for c in range(1, len(CHUNKS)):
             load_x(c)
 
         nc.vector.tensor_copy(v_plane[:], tab_scales[:].bitcast(U8).indirect(offsets[:]))
@@ -136,38 +145,51 @@ def tile_list_tabx_none_kernel(tc, tab, w4_words, w4_scales, x, u, offs, out):
                 tab_words[:].bitcast(U32).indirect(offsets[:, h * 32 : (h + 1) * 32]),
             )
 
-        for h in range(3):
+        def finish_pair(g):
+            x_pass(g, 0, 128)
+            table_pass(g, 128, 256)
+            x_pass(g, 128, 256)
+
+        for h in range(2):
             gather_words(h)
             table_pass(h)
+        gather_words(2)
+        table_pass(2, 0, 128)
+        table_pass(3, 0, 128)
         for c in range(7):
             cast_x(on_scalar, c)
         quantize_x(0, 512)
         x_pass(0)
         gather_words(3)
-        for g in range(3, 7):
+        for g in range(4, 8):
             table_pass(g)
-        empty(on_vector, 0)
-        store(0, 512)
         quantize_x(512, 512)
         x_pass(1)
+        empty(on_vector, 0)
+        store(0, 512)
         quantize_x(1024, 256)
+        finish_pair(2)
         empty(on_vector, 1)
-        store(512, 512)
+        store(1, 512)
         quantize_x(1280, 256)
-        x_pass(2)
-        cast_x(on_vector, 7, 0, LAST_SPLIT)
-        cast_x(on_scalar, 7, LAST_SPLIT, CHUNK)
+        finish_pair(3)
+        cast_x(on_vector, 7)
+        cast_x(on_vector, 8, 0, LAST_SPLIT)
+        cast_x(on_scalar, 8, LAST_SPLIT)
         quantize_x(1536, 256)
-        x_pass(3)
         x_pass(4)
-        quantize_x(1792, 256)
         x_pass(5)
+        quantize_x(1792, 128)
         x_pass(6)
+        quantize_x(1920, 128)
+        x_pass(7)
         empty(on_scalar, 2)
-        store(1024, 512)
+        store(2, 256)
         empty(on_scalar, 3)
+        store(3, 256)
         empty(on_vector, 4)
-        store(1536, 256)
-        empty(on_scalar, 5)
-        empty(on_vector, 6)
-        store(1792, 256)
+        empty(on_vector, 5)
+        store(4, 256)
+        empty(on_scalar, 6)
+        empty(on_vector, 7)
+        store(6, 256)

from contextlib import ExitStack

import concourse.mybir as mybir

K, L, M, T, S = 512, 512, 128, 4096, 2048
FLOPS = 2 * (K + L) * M * S

F32 = mybir.dt.float32
BF16 = mybir.dt.bfloat16
I32 = mybir.dt.int32
U32 = mybir.dt.uint32
U16 = mybir.dt.uint16
U8 = mybir.dt.uint8
FP8X4 = mybir.dt.float8_e4m3fn_x4
FP4X4 = mybir.dt.float4_e2m1fn_x4

P = 128
PACK = 4
CHUNKS = [(0, 256), (256, 256), (512, 256), (768, 256), (1024, 256), (1280, 256), (1536, 256), (1792, 128), (1920, 128)]
BANKS = [(0, 512), (512, 512), (1024, 256), (1280, 256), (1536, 128), (1664, 128), (1792, 128), (1920, 128)]
LAST_SPLIT = 80
STAGE = [4 * 768, 4 * 1024, 4 * 1920, 4 * 1920 + 256, 4 * 1536, 4 * 1536 + 128, 4 * 1792, 4 * 1792 + 128]


def tile_list_tabx_none_kernel(tc, tab, w4_words, w4_scales, x, u, offs, out):
    nc = tc.nc
    with ExitStack() as ctx:
        keep = ctx.enter_context(tc.tile_pool(name="keep", bufs=1))
        psum = ctx.enter_context(tc.psum_pool(name="psum", bufs=1))

        offsets = keep.tile([P, S // 16], U16, name="offsets")
        tab_words = keep.tile([P, T], I32, name="tab_words", align_bytes=64)
        tab_scales = keep.tile([P, T // 4], I32, name="tab_scales", align_bytes=64)
        w4_codes = keep.tile([P, M // 2], I32, name="w4_codes", align_bytes=64)
        w4_plane = keep.tile([P, M // 4], I32, name="w4_plane", align_bytes=64)
        u_raw = keep.tile([P, PACK, M], F32, name="u_raw", align_bytes=64)
        u_bf = keep.tile([P, M, PACK], BF16, name="u_bf", align_bytes=64)
        u_codes = keep.tile([P, M], U32, name="u_codes", align_bytes=64)
        u_plane = keep.tile([P, M], U8, name="u_plane", align_bytes=64)
        x_all = keep.tile([P, PACK * S], F32, name="x_all", align_bytes=64)
        x_raw = [
            x_all[:, PACK * first : PACK * (first + width)].rearrange("p (j s) -> p j s", j=PACK)
            for first, width in CHUNKS
        ]
        x_bf = keep.tile([P, S, PACK], BF16, name="x_bf", align_bytes=64)
        x_codes = keep.tile([P, S], U32, name="x_codes", align_bytes=64)
        x_plane = keep.tile([P, S], U8, name="x_plane", align_bytes=64)
        v_codes = keep.tile([P, S], U32, name="v_codes", align_bytes=64)
        v_plane = keep.tile([P, S], U8, name="v_plane", align_bytes=64)
        acc = [psum.tile([P, width], F32, name=f"acc{g}") for g, (first, width) in enumerate(BANKS)]

        x_rows = x.rearrange("(p j) s -> p j s", j=PACK)
        words_hbm = tab[0, 0 : K * T].rearrange("(p b) -> p b", p=P).bitcast(I32)
        scales_hbm = tab[0, K * T : K * T + 16 * T].rearrange("(q r t) -> r q t", q=4, r=4).bitcast(I32)
        w4_scales_hbm = w4_scales[0].rearrange("(q r) n -> r q n", r=4).bitcast(I32)

        def load_x(c):
            first, width = CHUNKS[c]
            nc.sync.dma_start(out=x_raw[c], in_=x_rows[:, :, first : first + width])

        def interleave(copy, dst, src):
            copy(
                out=dst.rearrange("p (c i) t -> p c t i", i=4),
                in_=src.rearrange("p t (c i) -> p c t i", i=4),
            )

        def cast_x(copy, c, lo=0, hi=None):
            first, width = CHUNKS[c]
            hi = width if hi is None else hi
            interleave(copy, x_bf[:, first + lo : first + hi, :], x_raw[c][:, :, lo:hi])

        def quantize_x(first, width):
            cols = slice(first, first + width)
            nc.vector.quantize_mx(
                out=x_codes[:, cols].bitcast(FP8X4),
                scales=x_plane[:, cols],
                in_=x_bf[:, cols, :].rearrange("p w t -> p (w t)"),
            )

        def table_pass(g, lo=0, hi=None):
            first, width = BANKS[g]
            hi = width if hi is None else hi
            cols = slice(first + lo, first + hi)
            nc.tensor.matmul_mx(
                out=acc[g][:, lo:hi],
                lhsT=w4_codes[:].bitcast(U8).bitcast(FP4X4),
                lhsT_scale=w4_plane[:].bitcast(U8),
                rhs=v_codes[:, cols].bitcast(FP8X4),
                rhs_scale=v_plane[:, cols],
                start=True,
                stop=False,
            )

        def x_pass(g, lo=0, hi=None):
            first, width = BANKS[g]
            hi = width if hi is None else hi
            cols = slice(first + lo, first + hi)
            nc.tensor.matmul_mx(
                out=acc[g][:, lo:hi],
                lhsT=u_codes[:].bitcast(FP8X4),
                lhsT_scale=u_plane[:],
                rhs=x_codes[:, cols].bitcast(FP8X4),
                rhs_scale=x_plane[:, cols],
                start=False,
                stop=True,
            )

        def empty(copy, g):
            first, width = BANKS[g]
            copy(out=x_all[:, STAGE[g] : STAGE[g] + width], in_=acc[g][:])

        def store(g, width):
            first = BANKS[g][0]
            nc.sync.dma_start(out=out[:, first : first + width], in_=x_all[:, STAGE[g] : STAGE[g] + width])

        on_vector = nc.vector.tensor_copy
        on_scalar = nc.scalar.copy

        nc.vector.memset(tab_scales[:], 0)
        nc.vector.memset(tab_words[:, 0:8], 0)
        nc.vector.memset(x_all[:].rearrange("p (c s) -> p c s", s=512)[:, :, 0:8], 0.0)
        nc.vector.memset(w4_plane[:], 0)

        nc.sync.dma_start(offsets[:], offs)
        nc.sync.dma_start(out=u_raw[:], in_=u.rearrange("(p j) n -> p j n", j=PACK))
        nc.sync.dma_start(out=w4_codes[:], in_=w4_words[0].bitcast(I32))
        for r in range(4):
            nc.sync.dma_start(out=tab_scales[r:P:32, :], in_=scales_hbm[r])
        nc.sync.dma_start(out=tab_words[:], in_=words_hbm)
        load_x(0)
        for r in range(4):
            nc.sync.dma_start(out=w4_plane[r:P:32, :], in_=w4_scales_hbm[r])
        for c in range(1, len(CHUNKS)):
            load_x(c)

        nc.vector.tensor_copy(v_plane[:], tab_scales[:].bitcast(U8).indirect(offsets[:]))
        interleave(on_scalar, u_bf[:], u_raw[:])
        nc.vector.quantize_mx(
            out=u_codes[:].bitcast(FP8X4), scales=u_plane[:], in_=u_bf[:].rearrange("p w t -> p (w t)")
        )

        def gather_words(h):
            nc.vector.tensor_copy(
                v_codes[:, h * 512 : (h + 1) * 512],
                tab_words[:].bitcast(U32).indirect(offsets[:, h * 32 : (h + 1) * 32]),
            )

        def finish_pair(g):
            x_pass(g, 0, 128)
            table_pass(g, 128, 256)
            x_pass(g, 128, 256)

        for h in range(2):
            gather_words(h)
            table_pass(h)
        gather_words(2)
        table_pass(2, 0, 128)
        table_pass(3, 0, 128)
        for c in range(7):
            cast_x(on_scalar, c)
        quantize_x(0, 512)
        x_pass(0)
        gather_words(3)
        for g in range(4, 8):
            table_pass(g)
        quantize_x(512, 512)
        x_pass(1)
        empty(on_vector, 0)
        store(0, 512)
        quantize_x(1024, 256)
        finish_pair(2)
        empty(on_vector, 1)
        store(1, 512)
        quantize_x(1280, 256)
        finish_pair(3)
        cast_x(on_vector, 7)
        cast_x(on_vector, 8, 0, LAST_SPLIT)
        cast_x(on_scalar, 8, LAST_SPLIT)
        quantize_x(1536, 256)
        x_pass(4)
        x_pass(5)
        quantize_x(1792, 128)
        x_pass(6)
        quantize_x(1920, 128)
        x_pass(7)
        empty(on_scalar, 2)
        store(2, 256)
        empty(on_scalar, 3)
        store(3, 256)
        empty(on_vector, 4)
        empty(on_vector, 5)
        store(4, 256)
        empty(on_scalar, 6)
        empty(on_vector, 7)
        store(6, 256)
